import numpy as np
import ml_dtypes


def mxq(x, axis, fmt="e4m3"):
    dtype, down = {"e4m3": (ml_dtypes.float8_e4m3fn, 7), "e5m2": (ml_dtypes.float8_e5m2, 14)}[fmt]
    v = np.moveaxis(np.asarray(x, np.float32).astype(ml_dtypes.bfloat16).astype(np.float64), axis, -1)
    blocks = v.reshape(v.shape[:-1] + (-1, 32))
    amax = np.abs(blocks).max(-1, keepdims=True)
    byte = np.maximum(np.where(amax > 0, np.frexp(amax)[1] - 1 + 127, 0) - down, 1)
    scale = np.exp2(byte - 127.0)
    codes = (blocks / scale).astype(np.float32).astype(dtype).astype(np.float64)
    return np.moveaxis((codes * scale).reshape(v.shape), -1, axis)


WIDE = False


def mx_kscale(k):
    if not WIDE:
        return np.ones(k)
    levels = np.array([30, -30])
    if k % 512:
        return np.exp2(np.random.permutation(np.resize(levels, k // 32))).repeat(32)
    a = np.empty((k // 512, 16))
    for p in range(k // 512):
        a[p, :8] = np.random.permutation(np.resize(levels, 8))
        for g in range(8):
            far = levels[np.abs(levels - a[p, g]) >= 10]
            a[p, g + 8] = far[np.random.randint(len(far))]
    return np.exp2(a.ravel()).repeat(32)


def f64(x):
    return np.asarray(x).astype(np.float64)


def striped(idx):
    return np.tile(np.asarray(idx).reshape(-1, 16).T, (8, 1)).astype(np.uint16)


def unstriped(offs):
    return offs[:16].T.reshape(-1).astype(np.int64)


E2M1 = np.array([0.0, 0.5, 1.0, 1.5, 2.0, 3.0, 4.0, 6.0, -0.0, -0.5, -1.0, -1.5, -2.0, -3.0, -4.0, -6.0])


def pack_weight(w, fmt):
    k, n = w.shape
    w = f64(np.asarray(w, np.float32).astype(ml_dtypes.bfloat16)).reshape(k // 32, 32, n)
    amax = np.abs(w).max(1)
    if fmt in ("e4m3", "e5m2"):
        byte = np.frexp(amax)[1] - 1 + 127 - (7 if fmt == "e4m3" else 14)
    else:
        mant, ex = np.frexp(amax / 6.0)
        byte = np.where(mant > 0.5, ex, ex - 1) + 127
    byte = np.clip(np.where(amax > 0, byte, 1), 1, 254)
    scaled = (w * np.exp2(127.0 - byte)[:, None, :]).reshape(k, n).astype(np.float32)
    by_word = np.ascontiguousarray(scaled.reshape(k // 512, 128, 4, n).transpose(0, 1, 3, 2))
    if fmt in ("e4m3", "e5m2"):
        words = by_word.astype(ml_dtypes.float8_e4m3fn if fmt == "e4m3" else ml_dtypes.float8_e5m2).view(np.uint8)
    else:
        c = by_word.astype(ml_dtypes.float4_e2m1fn).view(np.uint8) & 0xF
        words = (c[..., 0::2] | (c[..., 1::2] << 4)).reshape(k // 512, 128, 2 * n)
    return np.ascontiguousarray(words), np.ascontiguousarray(byte.astype(np.uint8).reshape(k // 512, 16, n))


def unpack_weight(words, scales, fmt):
    g, _, n = scales.shape
    words = np.ascontiguousarray(words).reshape(g, 128, n, -1)
    if fmt in ("e4m3", "e5m2"):
        vals = words.view(ml_dtypes.float8_e4m3fn if fmt == "e4m3" else ml_dtypes.float8_e5m2).astype(np.float64)
    else:
        nib = np.empty((g, 128, n, 4), np.uint8)
        nib[..., 0::2] = words & 0xF
        nib[..., 1::2] = words >> 4
        vals = E2M1[nib]
    vals = vals * np.repeat(np.exp2(scales.astype(np.float64) - 127.0), 8, axis=1)[..., None]
    return vals.transpose(0, 1, 3, 2).reshape(g * 512, n)


K, T, J, R, O, N, L, E = 512, 2048, 256, 512, 128, 256, 512, 1024


def setup_inputs():
    n = np.random.standard_normal
    idx = np.random.permutation(T)[:J]
    idx2 = np.random.permutation(T)[:J]
    idx3 = np.random.permutation(T)[:J]
    idx4 = np.random.permutation(J)[:O]
    idx5 = np.random.permutation(J)[:O]
    idx6 = np.random.permutation(E)[:O]
    fk = mx_kscale(K)
    fr = mx_kscale(R)
    fl = mx_kscale(L)
    xtp = pack_weight(n((K, T)) / fk[:, None], "e4m3")
    wp = pack_weight(n((K, R)) * 1 / np.sqrt(K) * fk[:, None] * fr, "e2m1")
    wbp = pack_weight(n((R, N)) * 1 / np.sqrt(R) / fr[:, None], "e5m2")
    sxp = pack_weight(n((L, O)) / fl[:, None], "e2m1")
    wsp = pack_weight(n((L, N)) * 1 / np.sqrt(L) * fl[:, None], "e5m2")
    return {
        "xt_words": xtp[0],
        "xt_scales": xtp[1],
        "w_words": wp[0],
        "w_scales": wp[1],
        "wb_words": wbp[0],
        "wb_scales": wbp[1],
        "sx_words": sxp[0],
        "sx_scales": sxp[1],
        "ws_words": wsp[0],
        "ws_scales": wsp[1],
        "offs": striped(idx),
        "offs2": striped(idx2),
        "offs3": striped(idx3),
        "offs4": striped(idx4),
        "offs5": striped(idx5),
        "offs6": striped(idx6),
    }


def reference(xt_words, xt_scales, w_words, w_scales, wb_words, wb_scales, sx_words, sx_scales, ws_words, ws_scales, offs, offs2, offs3, offs4, offs5, offs6):
    idx = unstriped(offs)
    idx2 = unstriped(offs2)
    idx3 = unstriped(offs3)
    idx4 = unstriped(offs4)
    idx5 = unstriped(offs5)
    idx6 = unstriped(offs6)
    xtu = unpack_weight(xt_words, xt_scales, "e4m3")
    wu = unpack_weight(w_words, w_scales, "e2m1")
    wbu = unpack_weight(wb_words, wb_scales, "e5m2")
    sxu = unpack_weight(sx_words, sx_scales, "e2m1")
    wsu = unpack_weight(ws_words, ws_scales, "e5m2")
    xtidxg = xtu[:, idx]
    a = wu.T @ xtidxg
    xtidx2g = xtu[:, idx2]
    b = wu.T @ xtidx2g
    xtidx3g = xtu[:, idx3]
    g0 = wu.T @ xtidx3g
    c1 = np.maximum(b, g0)
    hid = np.abs(a[:, idx4] - c1[:, idx5])
    hidq = mxq(hid, 0, "e4m3")
    p = wbu.T @ hidq + wsu.T @ sxu
    y = np.zeros((N, E))
    y[:, idx6] = p
    return y

@@ -1,0 +1,197 @@
+from contextlib import ExitStack
+
+import concourse.mybir as mybir
+
+K, T, J, R, O, N, L, E = 512, 2048, 256, 512, 128, 256, 512, 1024
+FLOPS = 2 * K * R * J * 3 + 2 * R * N * O + 2 * L * N * O
+
+F32 = mybir.dt.float32
+BF16 = mybir.dt.bfloat16
+I32 = mybir.dt.int32
+U32 = mybir.dt.uint32
+U16 = mybir.dt.uint16
+U8 = mybir.dt.uint8
+E4M3 = mybir.dt.float8_e4m3fn_x4
+E5M2 = mybir.dt.float8_e5m2_x4
+E2M1 = mybir.dt.float4_e2m1fn_x4
+ALU = mybir.AluOpType
+ACT = mybir.ActivationFunctionType
+P = 128
+SPLIT = 80
+
+
+def load_plane_rows(queue, plane, scales, quadrants=range(4)):
+    for q in quadrants:
+        queue.dma_start(out=plane[32 * q : 32 * q + 4, :].bitcast(I32), in_=scales[0, 4 * q : 4 * q + 4, :].bitcast(I32))
+
+
+def tile_list_triple_looked_skip_scattered_kernel(
+    tc, xt_words, xt_scales, w_words, w_scales, wb_words, wb_scales, sx_words, sx_scales, ws_words, ws_scales,
+    offs, offs2, offs3, offs4, offs5, offs6, out,
+):
+    nc = tc.nc
+    with ExitStack() as ctx:
+        sb = ctx.enter_context(tc.tile_pool(name="sb", bufs=1))
+        big = ctx.enter_context(tc.tile_pool(name="big", bufs=1))
+        ps = ctx.enter_context(tc.psum_pool(name="ps", bufs=1))
+
+        def tile(shape, dtype, name):
+            return sb.tile(shape, dtype, name=name, align_bytes=64)
+
+        def bank(index, width, name):
+            return ps.tile([P, width], F32, name=name, tag="bank%d" % index)
+
+        list_a = tile([P, J // 16], U16, "list_a")
+        list_b = tile([P, J // 16], U16, "list_b")
+        list_g = tile([P, J // 16], U16, "list_g")
+        list_pick_a = tile([P, O // 16], U16, "list_pick_a")
+        list_pick_c = tile([P, O // 16], U16, "list_pick_c")
+        list_place = tile([P, O // 16], U16, "list_place")
+
+        x_words = big.tile([P, T], U32, name="x_words", offset=0)
+        x_plane = tile([P, T], U8, "x_plane")
+        w_raw = tile([P, 2 * R], U8, "w_raw")
+        w_raw_plane = sb.tile([P, R], U8, name="w_raw_plane", tag="reused", align_bytes=64)
+        planes = tile([P, 2 * N + O], U8, "planes")
+        wb_plane = planes[:, 0:N]
+        ws_plane = planes[:, N : 2 * N]
+        sx_plane = planes[:, 2 * N : 2 * N + O]
+        w_dealt = tile([P, 2 * R], U8, "w_dealt")
+        w_plane = tile([P, R], U8, "w_plane")
+        wb_codes = tile([P, N], U32, "wb_codes")
+        ws_codes = tile([P, N], U32, "ws_codes")
+        sx_codes = tile([P, 2 * O], U8, "sx_codes")
+
+        nc.gpsimd.dma_start(out=x_words[:].bitcast(I32), in_=xt_words[0].rearrange("p c r -> p (c r)").bitcast(I32))
+        nc.vector.memset(x_plane[:].bitcast(I32), 0)
+        nc.vector.memset(w_raw_plane[:].bitcast(I32), 0)
+        nc.vector.memset(planes[:].bitcast(I32), 0)
+        load_plane_rows(nc.scalar, x_plane, xt_scales, (0, 1))
+        load_plane_rows(nc.sync, x_plane, xt_scales, (2, 3))
+        nc.sync.dma_start(list_b[:], offs2)
+        nc.sync.dma_start(list_g[:], offs3)
+        nc.sync.dma_start(out=w_raw[:].bitcast(I32), in_=w_words[0].bitcast(I32))
+        nc.sync.dma_start(list_a[:], offs)
+        load_plane_rows(nc.sync, w_raw_plane, w_scales)
+        nc.sync.dma_start(list_pick_c[:], offs5)
+        nc.sync.dma_start(list_pick_a[:], offs4)
+        load_plane_rows(nc.sync, sx_plane, sx_scales)
+        load_plane_rows(nc.sync, ws_plane, ws_scales)
+        load_plane_rows(nc.sync, wb_plane, wb_scales)
+        nc.sync.dma_start(out=sx_codes[:].bitcast(I32), in_=sx_words[0].bitcast(I32))
+        nc.sync.dma_start(out=ws_codes[:].bitcast(I32), in_=ws_words[0].rearrange("p c r -> p (c r)").bitcast(I32))
+        nc.sync.dma_start(out=wb_codes[:].bitcast(I32), in_=wb_words[0].rearrange("p c r -> p (c r)").bitcast(I32))
+        nc.sync.dma_start(list_place[:], offs6)
+
+        def gather_bytes(name, picks):
+            got = tile([P, J], U8, name)
+            nc.vector.tensor_copy(out=got[:], in_=x_plane[:].indirect(picks[:]))
+            return got
+
+        def gather_words(got, picks):
+            nc.vector.tensor_copy(out=got, in_=x_words[:].indirect(picks[:]))
+            return got
+
+        def first_product(acc, t, codes, plane):
+            nc.tensor.matmul_mx(
+                out=acc[:],
+                lhsT=w_dealt[:, 2 * P * t : 2 * P * (t + 1)].bitcast(E2M1),
+                lhsT_scale=w_plane[:, P * t : P * (t + 1)],
+                rhs=codes.bitcast(E4M3),
+                rhs_scale=plane[:],
+                start=True,
+                stop=True,
+            )
+
+        b_plane = gather_bytes("b_plane", list_b)
+        g_plane = gather_bytes("g_plane", list_g)
+        a_plane = gather_bytes("a_plane", list_a)
+        nc.vector.tensor_copy(
+            out=w_plane[:].rearrange("p (t m) -> p t m", t=4), in_=w_raw_plane[:].rearrange("p (m t) -> p t m", t=4)
+        )
+        nc.vector.tensor_copy(
+            out=w_dealt[:].bitcast(U16).rearrange("p (t m) -> p t m", t=4),
+            in_=w_raw[:].bitcast(U16).rearrange("p (m t) -> p t m", t=4),
+        )
+        picked_words = sb.tile([P, 3 * J], U32, name="picked_words", tag="reused", align_bytes=64)
+        b_codes = gather_words(picked_words[:, 0:J], list_b)
+        g_codes = gather_words(picked_words[:, J : 2 * J], list_g)
+        a_codes = gather_words(picked_words[:, 2 * J : 3 * J], list_a)
+
+        pages = [big.tile([P, E], F32, name="page%d" % h, offset=4 * E * h) for h in range(2)]
+        for page in pages:
+            nc.gpsimd.memset(page[:], 0.0)
+
+        b_rows = []
+        for t in range(4):
+            acc = bank(t, J, "b_acc%d" % t)
+            first_product(acc, t, b_codes, b_plane)
+            rows = tile([P, J], F32, "b_rows%d" % t)
+            nc.scalar.copy(out=rows[:], in_=acc[:])
+            b_rows.append(rows)
+        c_rows = []
+        for t in range(4):
+            acc = bank(4 + t, J, "g_acc%d" % t)
+            first_product(acc, t, g_codes, g_plane)
+            rows = tile([P, J], F32, "c_rows%d" % t)
+            nc.vector.tensor_tensor(out=rows[:], in0=acc[:], in1=b_rows[t][:], op=ALU.max)
+            c_rows.append(rows)
+        c_picked = [tile([P, O], F32, "c_picked%d" % t) for t in range(4)]
+        a_rows = [tile([P, J], F32, "a_rows%d" % t) for t in range(4)]
+        a_accs = [bank(t, J, "a_acc%d" % t) for t in range(4)]
+        for t in range(4):
+            first_product(a_accs[t], t, a_codes, a_plane)
+
+        def pick_c_on_scalar(t):
+            nc.scalar.activation(out=c_picked[t][:], in_=c_rows[t][:].indirect(list_pick_c[:]), func=ACT.Copy)
+
+        def empty_a(t):
+            nc.scalar.copy(out=a_rows[t][:], in_=a_accs[t][:])
+
+        pick_c_on_scalar(0)
+        pick_c_on_scalar(1)
+        empty_a(0)
+        empty_a(1)
+        pick_c_on_scalar(2)
+        empty_a(2)
+        empty_a(3)
+        nc.vector.tensor_copy(out=c_picked[3][:], in_=c_rows[3][:].indirect(list_pick_c[:]))
+        diff = tile([P, 4, O], F32, "diff")
+        for t in range(4):
+            nc.vector.tensor_tensor(
+                out=diff[:, t, :], in0=a_rows[t][:].indirect(list_pick_a[:]), in1=c_picked[t][:], op=ALU.subtract
+            )
+
+        hid = tile([P, O, 4], BF16, "hid")
+        woven = diff[:].rearrange("p t o -> p o t")
+        nc.scalar.activation(out=hid[:, :SPLIT, :], in_=woven[:, :SPLIT, :], func=ACT.Abs)
+        nc.vector.scalar_tensor_tensor(
+            out=hid[:, SPLIT:, :], in0=woven[:, SPLIT:, :], scalar=-1.0, in1=woven[:, SPLIT:, :],
+            op0=ALU.mult, op1=ALU.max,
+        )
+        hid_codes = tile([P, O], U32, "hid_codes")
+        hid_plane = tile([P, O], U8, "hid_plane")
+        nc.vector.quantize_mx(
+            out=hid_codes[:].bitcast(E4M3), scales=hid_plane[:], in_=hid[:].rearrange("p o t -> p (o t)")
+        )
+
+        for h in range(2):
+            cols = slice(P * h, P * (h + 1))
+            acc = bank(h, O, "p_acc%d" % h)
+            nc.tensor.matmul_mx(
+                out=acc[:], lhsT=ws_codes[:, cols].bitcast(E5M2), lhsT_scale=ws_plane[:, cols],
+                rhs=sx_codes[:].bitcast(E2M1), rhs_scale=sx_plane, start=True, stop=False,
+            )
+            nc.tensor.matmul_mx(
+                out=acc[:], lhsT=wb_codes[:, cols].bitcast(E5M2), lhsT_scale=wb_plane[:, cols],
+                rhs=hid_codes[:].bitcast(E4M3), rhs_scale=hid_plane[:], start=False, stop=True,
+            )
+            values = tile([P, O], F32, "p_rows%d" % h)
+            if h == 0:
+                nc.vector.tensor_copy(out=values[:], in_=acc[:])
+                nc.vector.tensor_copy(out=pages[h][:].indirect(list_place[:]), in_=values[:])
+                nc.sync.dma_start(out=out[cols, :], in_=pages[h][:])
+            else:
+                nc.scalar.copy(out=values[:], in_=acc[:])
+                nc.scalar.activation(out=pages[h][:].indirect(list_place[:]), in_=values[:], func=ACT.Copy)
+                nc.scalar.dma_start(out=out[cols, :], in_=pages[h][:])

@@ -49,7 +49,7 @@ def tile_list_triple_looked_skip_scattered_kernel(
         list_place = tile([P, O // 16], U16, "list_place")
 
         x_words = big.tile([P, T], U32, name="x_words", offset=0)
-        x_plane = tile([P, T], U8, "x_plane")
+        x_plane = sb.tile([P, T], U8, name="x_plane", tag="x_plane_then_b", align_bytes=64)
         w_raw = tile([P, 2 * R], U8, "w_raw")
         w_raw_plane = sb.tile([P, R], U8, name="w_raw_plane", tag="reused", align_bytes=64)
         planes = tile([P, 2 * N + O], U8, "planes")
@@ -66,11 +66,11 @@ def tile_list_triple_looked_skip_scattered_kernel(
         nc.vector.memset(x_plane[:].bitcast(I32), 0)
         nc.vector.memset(w_raw_plane[:].bitcast(I32), 0)
         nc.vector.memset(planes[:].bitcast(I32), 0)
+        nc.scalar.dma_start(out=w_raw[:].bitcast(I32), in_=w_words[0].bitcast(I32))
         load_plane_rows(nc.scalar, x_plane, xt_scales, (0, 1))
         load_plane_rows(nc.sync, x_plane, xt_scales, (2, 3))
         nc.sync.dma_start(list_b[:], offs2)
         nc.sync.dma_start(list_g[:], offs3)
-        nc.sync.dma_start(out=w_raw[:].bitcast(I32), in_=w_words[0].bitcast(I32))
         nc.sync.dma_start(list_a[:], offs)
         load_plane_rows(nc.sync, w_raw_plane, w_scales)
         nc.sync.dma_start(list_pick_c[:], offs5)
@@ -107,16 +107,16 @@ def tile_list_triple_looked_skip_scattered_kernel(
         g_plane = gather_bytes("g_plane", list_g)
         a_plane = gather_bytes("a_plane", list_a)
         nc.vector.tensor_copy(
-            out=w_plane[:].rearrange("p (t m) -> p t m", t=4), in_=w_raw_plane[:].rearrange("p (m t) -> p t m", t=4)
-        )
-        nc.vector.tensor_copy(
             out=w_dealt[:].bitcast(U16).rearrange("p (t m) -> p t m", t=4),
             in_=w_raw[:].bitcast(U16).rearrange("p (m t) -> p t m", t=4),
         )
-        picked_words = sb.tile([P, 3 * J], U32, name="picked_words", tag="reused", align_bytes=64)
-        b_codes = gather_words(picked_words[:, 0:J], list_b)
-        g_codes = gather_words(picked_words[:, J : 2 * J], list_g)
-        a_codes = gather_words(picked_words[:, 2 * J : 3 * J], list_a)
+        b_words = sb.tile([P, J], U32, name="b_words", tag="x_plane_then_b", align_bytes=64)
+        b_codes = gather_words(b_words[:], list_b)
+        for t in range(4):
+            nc.vector.tensor_copy(out=w_plane[:, P * t : P * (t + 1)], in_=w_raw_plane[:, t::4])
+        picked_words = sb.tile([P, 2 * J], U32, name="picked_words", tag="reused", align_bytes=64)
+        g_codes = gather_words(picked_words[:, 0:J], list_g)
+        a_codes = gather_words(picked_words[:, J : 2 * J], list_a)
 
         pages = [big.tile([P, E], F32, name="page%d" % h, offset=4 * E * h) for h in range(2)]
         for page in pages:

@@ -18,6 +18,7 @@ ALU = mybir.AluOpType
 ACT = mybir.ActivationFunctionType
 P = 128
 SPLIT = 80
+EARLY = 768
 
 
 def load_plane_rows(queue, plane, scales, quadrants=range(4)):
@@ -32,7 +33,6 @@ def tile_list_triple_looked_skip_scattered_kernel(
     nc = tc.nc
     with ExitStack() as ctx:
         sb = ctx.enter_context(tc.tile_pool(name="sb", bufs=1))
-        big = ctx.enter_context(tc.tile_pool(name="big", bufs=1))
         ps = ctx.enter_context(tc.psum_pool(name="ps", bufs=1))
 
         def tile(shape, dtype, name):
@@ -48,8 +48,8 @@ def tile_list_triple_looked_skip_scattered_kernel(
         list_pick_c = tile([P, O // 16], U16, "list_pick_c")
         list_place = tile([P, O // 16], U16, "list_place")
 
-        x_words = big.tile([P, T], U32, name="x_words", offset=0)
-        x_plane = sb.tile([P, T], U8, name="x_plane", tag="x_plane_then_b", align_bytes=64)
+        x_words = tile([P, T], U32, "x_words")
+        x_plane = tile([P, T], U8, "x_plane")
         w_raw = tile([P, 2 * R], U8, "w_raw")
         w_raw_plane = sb.tile([P, R], U8, name="w_raw_plane", tag="reused", align_bytes=64)
         planes = tile([P, 2 * N + O], U8, "planes")
@@ -62,17 +62,22 @@ def tile_list_triple_looked_skip_scattered_kernel(
         ws_codes = tile([P, N], U32, "ws_codes")
         sx_codes = tile([P, 2 * O], U8, "sx_codes")
 
-        nc.gpsimd.dma_start(out=x_words[:].bitcast(I32), in_=xt_words[0].rearrange("p c r -> p (c r)").bitcast(I32))
         nc.vector.memset(x_plane[:].bitcast(I32), 0)
         nc.vector.memset(w_raw_plane[:].bitcast(I32), 0)
         nc.vector.memset(planes[:].bitcast(I32), 0)
-        nc.scalar.dma_start(out=w_raw[:].bitcast(I32), in_=w_words[0].bitcast(I32))
+        pages = [tile([P, E], F32, "page%d" % h) for h in range(2)]
+        for page in pages:
+            nc.vector.memset(page[:], 0.0)
+        token_words = xt_words[0].rearrange("p c r -> p (c r)").bitcast(I32)
+        nc.sync.dma_start(list_b[:], offs2)
+        nc.scalar.dma_start(out=x_words[:, :EARLY].bitcast(I32), in_=token_words[:, :EARLY])
         load_plane_rows(nc.scalar, x_plane, xt_scales, (0, 1))
         load_plane_rows(nc.sync, x_plane, xt_scales, (2, 3))
-        nc.sync.dma_start(list_b[:], offs2)
         nc.sync.dma_start(list_g[:], offs3)
-        nc.sync.dma_start(list_a[:], offs)
+        nc.scalar.dma_start(out=x_words[:, EARLY:].bitcast(I32), in_=token_words[:, EARLY:])
+        nc.sync.dma_start(out=w_raw[:].bitcast(I32), in_=w_words[0].bitcast(I32))
         load_plane_rows(nc.sync, w_raw_plane, w_scales)
+        nc.sync.dma_start(list_a[:], offs)
         nc.sync.dma_start(list_pick_c[:], offs5)
         nc.sync.dma_start(list_pick_a[:], offs4)
         load_plane_rows(nc.sync, sx_plane, sx_scales)
@@ -105,22 +110,18 @@ def tile_list_triple_looked_skip_scattered_kernel(
 
         b_plane = gather_bytes("b_plane", list_b)
         g_plane = gather_bytes("g_plane", list_g)
-        a_plane = gather_bytes("a_plane", list_a)
         nc.vector.tensor_copy(
             out=w_dealt[:].bitcast(U16).rearrange("p (t m) -> p t m", t=4),
             in_=w_raw[:].bitcast(U16).rearrange("p (m t) -> p t m", t=4),
         )
-        b_words = sb.tile([P, J], U32, name="b_words", tag="x_plane_then_b", align_bytes=64)
+        b_words = tile([P, J], U32, "b_words")
         b_codes = gather_words(b_words[:], list_b)
         for t in range(4):
             nc.vector.tensor_copy(out=w_plane[:, P * t : P * (t + 1)], in_=w_raw_plane[:, t::4])
         picked_words = sb.tile([P, 2 * J], U32, name="picked_words", tag="reused", align_bytes=64)
         g_codes = gather_words(picked_words[:, 0:J], list_g)
+        a_plane = gather_bytes("a_plane", list_a)
         a_codes = gather_words(picked_words[:, J : 2 * J], list_a)
-
-        pages = [big.tile([P, E], F32, name="page%d" % h, offset=4 * E * h) for h in range(2)]
-        for page in pages:
-            nc.gpsimd.memset(page[:], 0.0)
 
         b_rows = []
         for t in range(4):

from contextlib import ExitStack

import concourse.mybir as mybir

K, T, J, R, O, N, L, E = 512, 2048, 256, 512, 128, 256, 512, 1024
FLOPS = 2 * K * R * J * 3 + 2 * R * N * O + 2 * L * N * O

F32 = mybir.dt.float32
BF16 = mybir.dt.bfloat16
I32 = mybir.dt.int32
U32 = mybir.dt.uint32
U16 = mybir.dt.uint16
U8 = mybir.dt.uint8
E4M3 = mybir.dt.float8_e4m3fn_x4
E5M2 = mybir.dt.float8_e5m2_x4
E2M1 = mybir.dt.float4_e2m1fn_x4
ALU = mybir.AluOpType
ACT = mybir.ActivationFunctionType
P = 128
SPLIT = 80
EARLY = 768


def load_plane_rows(queue, plane, scales, quadrants=range(4)):
    for q in quadrants:
        queue.dma_start(out=plane[32 * q : 32 * q + 4, :].bitcast(I32), in_=scales[0, 4 * q : 4 * q + 4, :].bitcast(I32))


def tile_list_triple_looked_skip_scattered_kernel(
    tc, xt_words, xt_scales, w_words, w_scales, wb_words, wb_scales, sx_words, sx_scales, ws_words, ws_scales,
    offs, offs2, offs3, offs4, offs5, offs6, out,
):
    nc = tc.nc
    with ExitStack() as ctx:
        sb = ctx.enter_context(tc.tile_pool(name="sb", bufs=1))
        ps = ctx.enter_context(tc.psum_pool(name="ps", bufs=1))

        def tile(shape, dtype, name):
            return sb.tile(shape, dtype, name=name, align_bytes=64)

        def bank(index, width, name):
            return ps.tile([P, width], F32, name=name, tag="bank%d" % index)

        list_a = tile([P, J // 16], U16, "list_a")
        list_b = tile([P, J // 16], U16, "list_b")
        list_g = tile([P, J // 16], U16, "list_g")
        list_pick_a = tile([P, O // 16], U16, "list_pick_a")
        list_pick_c = tile([P, O // 16], U16, "list_pick_c")
        list_place = tile([P, O // 16], U16, "list_place")

        x_words = tile([P, T], U32, "x_words")
        x_plane = tile([P, T], U8, "x_plane")
        w_raw = tile([P, 2 * R], U8, "w_raw")
        w_raw_plane = sb.tile([P, R], U8, name="w_raw_plane", tag="reused", align_bytes=64)
        planes = tile([P, 2 * N + O], U8, "planes")
        wb_plane = planes[:, 0:N]
        ws_plane = planes[:, N : 2 * N]
        sx_plane = planes[:, 2 * N : 2 * N + O]
        w_dealt = tile([P, 2 * R], U8, "w_dealt")
        w_plane = tile([P, R], U8, "w_plane")
        wb_codes = tile([P, N], U32, "wb_codes")
        ws_codes = tile([P, N], U32, "ws_codes")
        sx_codes = tile([P, 2 * O], U8, "sx_codes")

        nc.vector.memset(x_plane[:].bitcast(I32), 0)
        nc.vector.memset(w_raw_plane[:].bitcast(I32), 0)
        nc.vector.memset(planes[:].bitcast(I32), 0)
        pages = [tile([P, E], F32, "page%d" % h) for h in range(2)]
        for page in pages:
            nc.vector.memset(page[:], 0.0)
        token_words = xt_words[0].rearrange("p c r -> p (c r)").bitcast(I32)
        nc.sync.dma_start(list_b[:], offs2)
        nc.scalar.dma_start(out=x_words[:, :EARLY].bitcast(I32), in_=token_words[:, :EARLY])
        load_plane_rows(nc.scalar, x_plane, xt_scales, (0, 1))
        load_plane_rows(nc.sync, x_plane, xt_scales, (2, 3))
        nc.sync.dma_start(list_g[:], offs3)
        nc.scalar.dma_start(out=x_words[:, EARLY:].bitcast(I32), in_=token_words[:, EARLY:])
        nc.sync.dma_start(out=w_raw[:].bitcast(I32), in_=w_words[0].bitcast(I32))
        load_plane_rows(nc.sync, w_raw_plane, w_scales)
        nc.sync.dma_start(list_a[:], offs)
        nc.sync.dma_start(list_pick_c[:], offs5)
        nc.sync.dma_start(list_pick_a[:], offs4)
        load_plane_rows(nc.sync, sx_plane, sx_scales)
        load_plane_rows(nc.sync, ws_plane, ws_scales)
        load_plane_rows(nc.sync, wb_plane, wb_scales)
        nc.sync.dma_start(out=sx_codes[:].bitcast(I32), in_=sx_words[0].bitcast(I32))
        nc.sync.dma_start(out=ws_codes[:].bitcast(I32), in_=ws_words[0].rearrange("p c r -> p (c r)").bitcast(I32))
        nc.sync.dma_start(out=wb_codes[:].bitcast(I32), in_=wb_words[0].rearrange("p c r -> p (c r)").bitcast(I32))
        nc.sync.dma_start(list_place[:], offs6)

        def gather_bytes(name, picks):
            got = tile([P, J], U8, name)
            nc.vector.tensor_copy(out=got[:], in_=x_plane[:].indirect(picks[:]))
            return got

        def gather_words(got, picks):
            nc.vector.tensor_copy(out=got, in_=x_words[:].indirect(picks[:]))
            return got

        def first_product(acc, t, codes, plane):
            nc.tensor.matmul_mx(
                out=acc[:],
                lhsT=w_dealt[:, 2 * P * t : 2 * P * (t + 1)].bitcast(E2M1),
                lhsT_scale=w_plane[:, P * t : P * (t + 1)],
                rhs=codes.bitcast(E4M3),
                rhs_scale=plane[:],
                start=True,
                stop=True,
            )

        b_plane = gather_bytes("b_plane", list_b)
        g_plane = gather_bytes("g_plane", list_g)
        nc.vector.tensor_copy(
            out=w_dealt[:].bitcast(U16).rearrange("p (t m) -> p t m", t=4),
            in_=w_raw[:].bitcast(U16).rearrange("p (m t) -> p t m", t=4),
        )
        b_words = tile([P, J], U32, "b_words")
        b_codes = gather_words(b_words[:], list_b)
        for t in range(4):
            nc.vector.tensor_copy(out=w_plane[:, P * t : P * (t + 1)], in_=w_raw_plane[:, t::4])
        picked_words = sb.tile([P, 2 * J], U32, name="picked_words", tag="reused", align_bytes=64)
        g_codes = gather_words(picked_words[:, 0:J], list_g)
        a_plane = gather_bytes("a_plane", list_a)
        a_codes = gather_words(picked_words[:, J : 2 * J], list_a)

        b_rows = []
        for t in range(4):
            acc = bank(t, J, "b_acc%d" % t)
            first_product(acc, t, b_codes, b_plane)
            rows = tile([P, J], F32, "b_rows%d" % t)
            nc.scalar.copy(out=rows[:], in_=acc[:])
            b_rows.append(rows)
        c_rows = []
        for t in range(4):
            acc = bank(4 + t, J, "g_acc%d" % t)
            first_product(acc, t, g_codes, g_plane)
            rows = tile([P, J], F32, "c_rows%d" % t)
            nc.vector.tensor_tensor(out=rows[:], in0=acc[:], in1=b_rows[t][:], op=ALU.max)
            c_rows.append(rows)
        c_picked = [tile([P, O], F32, "c_picked%d" % t) for t in range(4)]
        a_rows = [tile([P, J], F32, "a_rows%d" % t) for t in range(4)]
        a_accs = [bank(t, J, "a_acc%d" % t) for t in range(4)]
        for t in range(4):
            first_product(a_accs[t], t, a_codes, a_plane)

        def pick_c_on_scalar(t):
            nc.scalar.activation(out=c_picked[t][:], in_=c_rows[t][:].indirect(list_pick_c[:]), func=ACT.Copy)

        def empty_a(t):
            nc.scalar.copy(out=a_rows[t][:], in_=a_accs[t][:])

        pick_c_on_scalar(0)
        pick_c_on_scalar(1)
        empty_a(0)
        empty_a(1)
        pick_c_on_scalar(2)
        empty_a(2)
        empty_a(3)
        nc.vector.tensor_copy(out=c_picked[3][:], in_=c_rows[3][:].indirect(list_pick_c[:]))
        diff = tile([P, 4, O], F32, "diff")
        for t in range(4):
            nc.vector.tensor_tensor(
                out=diff[:, t, :], in0=a_rows[t][:].indirect(list_pick_a[:]), in1=c_picked[t][:], op=ALU.subtract
            )

        hid = tile([P, O, 4], BF16, "hid")
        woven = diff[:].rearrange("p t o -> p o t")
        nc.scalar.activation(out=hid[:, :SPLIT, :], in_=woven[:, :SPLIT, :], func=ACT.Abs)
        nc.vector.scalar_tensor_tensor(
            out=hid[:, SPLIT:, :], in0=woven[:, SPLIT:, :], scalar=-1.0, in1=woven[:, SPLIT:, :],
            op0=ALU.mult, op1=ALU.max,
        )
        hid_codes = tile([P, O], U32, "hid_codes")
        hid_plane = tile([P, O], U8, "hid_plane")
        nc.vector.quantize_mx(
            out=hid_codes[:].bitcast(E4M3), scales=hid_plane[:], in_=hid[:].rearrange("p o t -> p (o t)")
        )

        for h in range(2):
            cols = slice(P * h, P * (h + 1))
            acc = bank(h, O, "p_acc%d" % h)
            nc.tensor.matmul_mx(
                out=acc[:], lhsT=ws_codes[:, cols].bitcast(E5M2), lhsT_scale=ws_plane[:, cols],
                rhs=sx_codes[:].bitcast(E2M1), rhs_scale=sx_plane, start=True, stop=False,
            )
            nc.tensor.matmul_mx(
                out=acc[:], lhsT=wb_codes[:, cols].bitcast(E5M2), lhsT_scale=wb_plane[:, cols],
                rhs=hid_codes[:].bitcast(E4M3), rhs_scale=hid_plane[:], start=False, stop=True,
            )
            values = tile([P, O], F32, "p_rows%d" % h)
            if h == 0:
                nc.vector.tensor_copy(out=values[:], in_=acc[:])
                nc.vector.tensor_copy(out=pages[h][:].indirect(list_place[:]), in_=values[:])
                nc.sync.dma_start(out=out[cols, :], in_=pages[h][:])
            else:
                nc.scalar.copy(out=values[:], in_=acc[:])
                nc.scalar.activation(out=pages[h][:].indirect(list_place[:]), in_=values[:], func=ACT.Copy)
                nc.scalar.dma_start(out=out[cols, :], in_=pages[h][:])
